import numpy as np
import ml_dtypes


def mxq(x, axis, fmt="e4m3"):
    dtype, down = {"e4m3": (ml_dtypes.float8_e4m3fn, 7), "e5m2": (ml_dtypes.float8_e5m2, 14)}[fmt]
    v = np.moveaxis(np.asarray(x, np.float32).astype(ml_dtypes.bfloat16).astype(np.float64), axis, -1)
    blocks = v.reshape(v.shape[:-1] + (-1, 32))
    amax = np.abs(blocks).max(-1, keepdims=True)
    byte = np.maximum(np.where(amax > 0, np.frexp(amax)[1] - 1 + 127, 0) - down, 1)
    scale = np.exp2(byte - 127.0)
    codes = (blocks / scale).astype(np.float32).astype(dtype).astype(np.float64)
    return np.moveaxis((codes * scale).reshape(v.shape), -1, axis)


WIDE = False


def mx_kscale(k):
    if not WIDE:
        return np.ones(k)
    levels = np.array([30, -30])
    if k % 512:
        return np.exp2(np.random.permutation(np.resize(levels, k // 32))).repeat(32)
    a = np.empty((k // 512, 16))
    for p in range(k // 512):
        a[p, :8] = np.random.permutation(np.resize(levels, 8))
        for g in range(8):
            far = levels[np.abs(levels - a[p, g]) >= 10]
            a[p, g + 8] = far[np.random.randint(len(far))]
    return np.exp2(a.ravel()).repeat(32)


BF16 = ml_dtypes.bfloat16


def bf(x):
    return np.asarray(x, np.float32).astype(BF16)


def f64(x):
    return np.asarray(x).astype(np.float64)


E2M1 = np.array([0.0, 0.5, 1.0, 1.5, 2.0, 3.0, 4.0, 6.0, -0.0, -0.5, -1.0, -1.5, -2.0, -3.0, -4.0, -6.0])


def pack_weight(w, fmt):
    k, n = w.shape
    w = f64(bf(w)).reshape(k // 32, 32, n)
    amax = np.abs(w).max(1)
    if fmt in ("e4m3", "e5m2"):
        byte = np.frexp(amax)[1] - 1 + 127 - (7 if fmt == "e4m3" else 14)
    else:
        mant, ex = np.frexp(amax / 6.0)
        byte = np.where(mant > 0.5, ex, ex - 1) + 127
    byte = np.clip(np.where(amax > 0, byte, 1), 1, 254)
    scaled = (w * np.exp2(127.0 - byte)[:, None, :]).reshape(k, n).astype(np.float32)
    by_word = np.ascontiguousarray(scaled.reshape(k // 512, 128, 4, n).transpose(0, 1, 3, 2))
    if fmt in ("e4m3", "e5m2"):
        words = by_word.astype(ml_dtypes.float8_e4m3fn if fmt == "e4m3" else ml_dtypes.float8_e5m2).view(np.uint8)
    else:
        c = by_word.astype(ml_dtypes.float4_e2m1fn).view(np.uint8) & 0xF
        words = c[..., 0::2] | (c[..., 1::2] << 4)
    return np.ascontiguousarray(words), np.ascontiguousarray(byte.astype(np.uint8).reshape(k // 512, 16, n))


def unpack_weight(words, scales, fmt):
    g, p, n, _ = words.shape
    if fmt in ("e4m3", "e5m2"):
        vals = np.ascontiguousarray(words).view(ml_dtypes.float8_e4m3fn if fmt == "e4m3" else ml_dtypes.float8_e5m2).astype(np.float64)
    else:
        nib = np.empty((g, p, n, 4), np.uint8)
        nib[..., 0::2] = words & 0xF
        nib[..., 1::2] = words >> 4
        vals = E2M1[nib]
    vals = vals * np.repeat(np.exp2(scales.astype(np.float64) - 127.0), 8, axis=1)[..., None]
    return vals.transpose(0, 1, 3, 2).reshape(g * 512, n)

def planes(Y):
    n, m = Y.shape
    b = f64(bf(Y)).reshape(n // 32, 32, m)
    amax = np.abs(b).max(1)
    byte = np.clip(np.where(amax > 0, np.frexp(amax)[1] - 1 + 127 - 7, 1), 1, 254)
    codes = (b * np.exp2(127.0 - byte)[:, None, :]).reshape(n, m).astype(np.float32).astype(ml_dtypes.float8_e4m3fn).view(np.uint8)
    words = codes.reshape(n // 512, 128, 4, m).transpose(0, 1, 3, 2)
    return np.ascontiguousarray(words), np.ascontiguousarray(byte.astype(np.uint8).reshape(n // 512, 16, m))


S, T, P, D = 4, 1024, 512, 1024

def setup_inputs():
    s = mx_kscale(T)[:, None]
    weight = np.exp(0.5 * np.random.randn(S, T, 1))
    err = np.random.standard_t(3, size=(S, T, P)) / np.sqrt(T)
    G = weight * err
    x = np.random.randn(S, T, D)
    x[:, :, 0] = 1.0
    spread = np.exp(0.7 * np.random.randn(D))
    g_words, g_scales = pack_weight(f64(bf(G * s)).reshape(S * T, P), "e5m2")
    return {
        "g_words": g_words,
        "g_scales": g_scales,
        "x": bf(x / s),
        "prec": bf(np.exp(0.3 * np.random.randn(S, P))),
        "step": bf(0.5 * spread),
        "base": bf(0.5 * np.random.randn(P, D) * spread),
    }

def reference(g_words, g_scales, x, prec, step, base):
    G = unpack_weight(g_words, g_scales, "e5m2").reshape(S, T, P)
    xq = mxq(f64(x), 1, "e4m3")
    stat = G.swapaxes(1, 2) @ xq
    descent = stat * f64(prec)[:, :, None]
    y = f64(base)[None, :, :] + descent * f64(step)[None, None, :]
    Y = y.transpose(2, 0, 1).reshape(D, S * P)
    words, scales = planes(Y)
    return y, words, scales

from contextlib import ExitStack

import concourse.mybir as mybir
from concourse.masks import make_identity

S, T, NP, D = 4, 1024, 512, 1024
FLOPS = 2 * S * T * NP * D

F32 = mybir.dt.float32
BF16 = mybir.dt.bfloat16
U32 = mybir.dt.uint32
I32 = mybir.dt.int32
U8 = mybir.dt.uint8
E4M3X4 = mybir.dt.float8_e4m3fn_x4
E5M2X4 = mybir.dt.float8_e5m2_x4
ALU = mybir.AluOpType
ACT = mybir.ActivationFunctionType

P = 128
W = 512
UNITS = 8
LEAD = 3
V_COLS_HEAD = 256
V_COLS_FILL = 384
V_COLS = 192
ROUND = "v" * 28 + "ssvv"
COPY = "s" * 16
SPLIT_X = 2
ORDER = 0
SEQ = "QMUTIRY"
LU = 2
LT = 4
LY = 5
V_COLS_END = 192
END = 16


def tile_speaker_projection_step_k2_kernel(tc, g_words, g_scales, x, prec, step, base, out_0, out_1, out_2):
    nc = tc.nc
    with ExitStack() as ctx:
        keep = ctx.enter_context(tc.tile_pool(name="keep", bufs=1))
        work = ctx.enter_context(tc.tile_pool(name="work", bufs=2))
        psum = ctx.enter_context(tc.psum_pool(name="psum", bufs=2))
        ctx.enter_context(tc.manual_schedule())

        g_scale = keep.tile([P, 2 * S, W], U8, name="g_scale", align_bytes=64)
        y_scale = keep.tile([P, 2, S * W], U8, name="y_scale", align_bytes=64)
        rows = keep.tile([P, P], BF16, name="rows")
        factors = keep.tile([P, 24], F32, name="factors")
        ident_f = keep.tile([P, P], F32, name="ident_f")
        ident_b = keep.tile([P, P], BF16, name="ident_b")

        nc.vector.memset(g_scale[:].rearrange("p g n -> p (g n)").bitcast(I32), 0)
        nc.gpsimd.memset(rows[:], 0.0)
        nc.vector.memset(ident_b[:], 0.0)
        nc.vector.memset(ident_f[:], 0.0)
        nc.gpsimd.dma_start(out=rows[0:8, :], in_=step.rearrange("(c p) -> c p", p=P))
        nc.gpsimd.dma_start(out=rows[8:24, :], in_=prec.rearrange("a (b p) -> (a b) p", p=P))
        make_identity(nc, ident_b[:], nomemset=True)
        make_identity(nc, ident_f[:], nomemset=True)

        x_raw = {}
        g_code = {}

        def load_x(a, h, g0, g1):
            raw = keep.tile([P, 4, (g1 - g0) * W], BF16, name="x_raw_%d_%d_%d" % (a, h, g0))
            nc.sync.dma_start(
                out=raw[:], in_=x[a, W * h : W * (h + 1), W * g0 : W * g1].rearrange("(p t) d -> p t d", t=4)
            )
            for g in range(g0, g1):
                x_raw.setdefault((a, g, h), raw[:, :, W * (g - g0) : W * (g - g0 + 1)])

        def load_g(a):
            code = keep.tile([P, 2, W], U32, name="g_code_%d" % a, align_bytes=64)
            nc.sync.dma_start(
                out=code[:].bitcast(I32),
                in_=g_words[2 * a : 2 * a + 2].rearrange("h p n t -> p h (n t)").bitcast(I32),
            )
            g_code.setdefault(a, code)

        base_sb = {}

        def load_base(g):
            part = keep.tile([P, 4, W], BF16, name="base_%d" % g)
            nc.sync.dma_start(out=part[:], in_=base[:, W * g : W * (g + 1)].rearrange("(b p) d -> p b d", p=P))
            base_sb.setdefault(g, part)

        load_x(0, 0, 0, 1)
        load_x(0, 1, 0, 1)
        load_g(0)
        for q in range(4):
            nc.sync.dma_start(
                out=g_scale[32 * q : 32 * q + 4, :, :].bitcast(I32),
                in_=g_scales[:, 4 * q : 4 * q + 4, :].rearrange("g r n -> r g n").bitcast(I32),
            )
        load_x(0, 0, 1, 2)
        load_x(0, 1, 1, 2)
        load_base(0)
        for a in range(1, S):
            if a < SPLIT_X:
                load_x(a, 0, 0, 1)
                if a == 1 and ORDER == 1:
                    load_base(1)
                load_x(a, 1, 0, 1)
                if a == 1 and ORDER == 0:
                    load_base(1)
                load_g(a)
                load_x(a, 0, 1, 2)
                load_x(a, 1, 1, 2)
            else:
                load_x(a, 0, 0, 2)
                load_x(a, 1, 0, 2)
                load_g(a)

        x_side = {}
        x_code = {}
        scaled = {}
        updated = {}
        y_tile = {}
        y_pairs = {}
        y_side = {}
        y_code = {}

        def interleave(j, v_cols):
            a, g, h = j // 4, j // 2 % 2, j % 2
            side = work.tile([P, W, 4], BF16, name="x_side", bufs=3, align_bytes=64)
            src = x_raw[a, g, h].rearrange("p t (c i) -> p c t i", i=4)
            dst = side[:].rearrange("p (c i) t -> p c t i", i=4)
            cut = v_cols // 4
            nc.scalar.copy(out=dst[:, cut:], in_=src[:, cut:])
            nc.vector.tensor_copy(out=dst[:, :cut], in_=src[:, :cut])
            x_side.setdefault(j, side)

        def quantize_x(j):
            code = work.tile([P, W], U32, name="x_code", bufs=5, align_bytes=64)
            scale = work.tile([P, W], U8, name="x_scale", bufs=5, align_bytes=64)
            nc.vector.quantize_mx(
                out=code[:].bitcast(E4M3X4), scales=scale[:], in_=x_side[j][:].rearrange("p c t -> p (c t)")
            )
            x_code.setdefault(j, (code, scale))

        def product(k):
            u, half = divmod(k, 2)
            a, g = divmod(u, 2)
            banks = []
            for q in (2 * half, 2 * half + 1):
                bank = psum.tile([P, W], F32, name="mx_bank", bufs=3)
                for h in range(2):
                    code, scale = x_code[2 * u + h]
                    nc.tensor.matmul_mx(
                        out=bank[:],
                        lhsT=code[:, P * q : P * (q + 1)].bitcast(E4M3X4),
                        lhsT_scale=scale[:, P * q : P * (q + 1)],
                        rhs=g_code[a][:, h, :].bitcast(E5M2X4),
                        rhs_scale=g_scale[:, 2 * a + h, :],
                        start=(h == 0),
                        stop=(h == 1),
                    )
                z = work.tile([P, W], F32, name="scaled", bufs=4 + 2 * LU)
                c = 4 * g + q
                nc.scalar.activation(out=z[:], in_=bank[:], func=ACT.Copy, scale=factors[:, c : c + 1])
                scaled.setdefault((u, q), z)

        def update(k):
            u, half = divmod(k, 2)
            a, g = divmod(u, 2)
            for b in (2 * half, 2 * half + 1):
                bank = psum.tile([P, W], F32, name="turn_bank", bufs=3)
                for q in range(4):
                    nc.tensor.transpose(bank[:, P * q : P * (q + 1)], scaled[u, q][:, P * b : P * (b + 1)], ident_f[:])
                c = 8 + 4 * a + b
                y = work.tile([P, W], F32, name="y", bufs=14)
                nc.vector.scalar_tensor_tensor(
                    out=y[:],
                    in0=bank[:],
                    scalar=factors[:, c : c + 1],
                    in1=base_sb[g][:, b, :],
                    op0=ALU.mult,
                    op1=ALU.add,
                )
                nc.sync.dma_start(out=out_0[a, P * b : P * (b + 1), W * g : W * (g + 1)], in_=y[:])
                y_tile.setdefault((u, b), y)
                if ROUND[4 * u + b] == "g":
                    round_y(u, b, "g")

        def round_y(u, b, engine):
            pairs = work.tile([P, 2, P, 2], BF16, name="y_pairs", bufs=8)
            src = y_tile[u, b][:].rearrange("p (m v e) -> p v m e", v=2, e=2)
            if engine == "g":
                nc.gpsimd.tensor_scalar(out=pairs[:], in0=src, scalar1=1.0, scalar2=-0.0, op0=ALU.mult, op1=ALU.add)
            elif engine == "s":
                nc.scalar.copy(out=pairs[:], in_=src)
            else:
                nc.vector.tensor_copy(out=pairs[:], in_=src)
            y_pairs.setdefault((u, b), pairs)

        def turn_back(k):
            u, half = divmod(k, 2)
            side = work.tile([P, 2 * P, 4], BF16, name="y_side", bufs=3, align_bytes=64)
            y_side.setdefault(k, side)
            bank = psum.tile([P, 2, 2, P], F32, name="word_bank", bufs=2)
            for bb in range(2):
                words = y_pairs[u, 2 * half + bb][:].rearrange("p v m e -> p v (m e)").bitcast(F32)
                for v in range(2):
                    nc.tensor.transpose(bank[:, bb, v, :], words[:, v, :], ident_f[:])
            dst = side[:].bitcast(F32).rearrange("p (b r) v -> p b r v", b=2)
            src = bank[:].rearrange("p b v r -> p b r v")
            if COPY[k] == "v":
                nc.vector.tensor_copy(out=dst, in_=src)
            else:
                nc.scalar.copy(out=dst, in_=src)

        def store_scales(a0, a1):
            for q in range(4):
                nc.sync.dma_start(
                    out=out_2[:, 4 * q : 4 * q + 4, W * a0 : W * a1].rearrange("g r m -> r g m").bitcast(I32),
                    in_=y_scale[32 * q : 32 * q + 4, :, W * a0 : W * a1].bitcast(I32),
                )

        def quantize_y(k):
            u, half = divmod(k, 2)
            a, g = divmod(u, 2)
            if half == 0:
                fresh = work.tile([P, W], U32, name="y_code", bufs=4, align_bytes=64)
                y_code.setdefault(u, fresh)
            code = y_code[u]
            c0 = 2 * P * half
            nc.vector.quantize_mx(
                out=code[:, c0 : c0 + 2 * P].bitcast(E4M3X4),
                scales=y_scale[:, g, W * a + c0 : W * a + c0 + 2 * P],
                in_=y_side[k][:].rearrange("p c t -> p (c t)"),
            )
            if half == 0:
                return
            nc.sync.dma_start(
                out=out_1[g, :, W * a : W * (a + 1), :].rearrange("p m t -> p (m t)").bitcast(I32),
                in_=code[:].bitcast(I32),
            )
            if u == UNITS - 3:
                store_scales(0, S - 1)
            if u == UNITS - 1:
                store_scales(S - 1, S)

        halves = 2 * UNITS
        for k in range(-LEAD, halves + LY):
            if k == -1:
                turned = psum.tile([P, P], BF16, name="word_bank", bufs=2)
                nc.tensor.transpose(turned[:], rows[:], ident_b[:])
                nc.scalar.copy(out=factors[:], in_=turned[:, 0:24])
            for stage in SEQ:
                if stage == "M" and 0 <= k < halves:
                    product(k)
                if stage == "U" and 0 <= k - LU < halves:
                    update(k - LU)
                if stage == "T" and 0 <= k - LT < halves:
                    turn_back(k - LT)
                if stage == "Q" and 0 <= k + LEAD - 1 < halves:
                    quantize_x(k + LEAD - 1)
                if stage == "I" and k + LEAD < halves:
                    interleave(k + LEAD, V_COLS_HEAD if k < 0 else V_COLS_FILL if k < LU else V_COLS_END if k + LEAD >= END else V_COLS)
                if stage == "R" and 0 <= k - LU < halves:
                    for b in (2 * (k - LU), 2 * (k - LU) + 1):
                        if ROUND[b] != "g":
                            round_y(b // 4, b % 4, ROUND[b])
                if stage == "Y" and 0 <= k - LY < halves:
                    quantize_y(k - LY)
